import numpy as np
import ml_dtypes


def mxq(x, axis, fmt="e4m3"):
    dtype, down = {"e4m3": (ml_dtypes.float8_e4m3fn, 7), "e5m2": (ml_dtypes.float8_e5m2, 14)}[fmt]
    v = np.moveaxis(np.asarray(x, np.float32).astype(ml_dtypes.bfloat16).astype(np.float64), axis, -1)
    blocks = v.reshape(v.shape[:-1] + (-1, 32))
    amax = np.abs(blocks).max(-1, keepdims=True)
    byte = np.maximum(np.where(amax > 0, np.frexp(amax)[1] - 1 + 127, 0) - down, 1)
    scale = np.exp2(byte - 127.0)
    codes = (blocks / scale).astype(np.float32).astype(dtype).astype(np.float64)
    return np.moveaxis((codes * scale).reshape(v.shape), -1, axis)


WIDE = False


def mx_kscale(k):
    if not WIDE:
        return np.ones(k)
    levels = np.array([18, -18])
    if k % 512:
        return np.exp2(np.random.permutation(np.resize(levels, k // 32))).repeat(32)
    a = np.empty((k // 512, 16))
    for p in range(k // 512):
        a[p, :8] = np.random.permutation(np.resize(levels, 8))
        for g in range(8):
            far = levels[np.abs(levels - a[p, g]) >= 10]
            a[p, g + 8] = far[np.random.randint(len(far))]
    return np.exp2(a.ravel()).repeat(32)


def f64(x):
    return np.asarray(x).astype(np.float64)


def striped(idx):
    return np.tile(np.asarray(idx).reshape(-1, 16).T, (8, 1)).astype(np.uint16)


def unstriped(offs):
    return offs[:16].T.reshape(-1).astype(np.int64)


B, N, T, D, DV, NQ = 2, 512, 2048, 256, 1024, 512


def setup_inputs():
    n = np.random.standard_normal
    seg = T // B
    idx = np.concatenate([b * seg + np.random.permutation(seg)[:N] for b in range(B)])
    s = mx_kscale(DV)[:, None]
    z = mx_kscale(NQ)[:, None]
    p = np.exp(n((B, NQ, N)))
    p = p / p.mean(2, keepdims=True)
    return {
        "doT": (n((B, DV, NQ)) * s / np.sqrt(DV)).astype(np.float32),
        "vT": (n((DV, T)) / s).astype(np.float32),
        "p": (p * z / np.sqrt(NQ)).astype(np.float32),
        "delta": (0.3 * n((B, NQ, 1))).astype(np.float32),
        "qm": (n((B, NQ, D)) / z).astype(np.float32),
        "offs": striped(idx),
    }


def reference(doT, vT, p, delta, qm, offs):
    idx = unstriped(offs)
    pick = lambda x: x[:, idx].reshape(x.shape[0], B, N).transpose(1, 0, 2)
    dp = mxq(f64(doT), 1, "e5m2").transpose(0, 2, 1) @ mxq(pick(f64(vT)), 1, "e4m3")
    ds = f64(p) * (dp - f64(delta))
    dk = mxq(f64(qm), 1, "e4m3").transpose(0, 2, 1) @ mxq(ds, 1, "e5m2")
    out = np.zeros((D, T))
    out[:, idx] = dk.transpose(1, 0, 2).reshape(D, B * N)
    return out

@@ -1,0 +1,251 @@
+from contextlib import ExitStack
+
+import concourse.mybir as mybir
+
+B, N, T, D, DV, NQ = 2, 512, 2048, 256, 1024, 512
+FLOPS = 2 * B * NQ * N * (DV + D)
+BYTES = 4 * (B * DV * NQ + DV * B * N + B * NQ * N + B * NQ + B * NQ * D + D * T) + 2 * 128 * (B * N // 16)
+
+F32 = mybir.dt.float32
+BF16 = mybir.dt.bfloat16
+U32 = mybir.dt.uint32
+U16 = mybir.dt.uint16
+U8 = mybir.dt.uint8
+E4M3 = mybir.dt.float8_e4m3fn_x4
+E5M2 = mybir.dt.float8_e5m2_x4
+COPY = mybir.ActivationFunctionType.Copy
+IDENT = mybir.ActivationFunctionType.Identity
+ADD = mybir.AluOpType.add
+MUL = mybir.AluOpType.mult
+
+P = 128
+PACK = 4
+K_PASS = P * PACK
+SEG = T // B
+G = DV // K_PASS
+COLS = N // 16
+
+
+def move(nc, engine, out, in_):
+    if engine == "scalar":
+        nc.scalar.activation(out, in_, COPY)
+    elif engine == "vector":
+        nc.vector.tensor_copy(out, in_)
+    else:
+        nc.gpsimd.tensor_scalar(out, in_, 1.0, 0.0, MUL, ADD)
+
+
+def share(width, vec, gps=0.0):
+    v = int(width * vec) // 8 * 8
+    g = int(width * gps) // 8 * 8
+    s = width - v - g
+    return [x for x in [("scalar", 0, s), ("vector", s, s + v), ("gpsimd", s + v, width)] if x[1] < x[2]]
+
+
+def tile_attend_bwd_seg_kernel(tc, doT, vT, p, delta, qm, offs, out):
+    nc = tc.nc
+    with ExitStack() as ctx:
+        hold = ctx.enter_context(tc.tile_pool(name="hold", bufs=1))
+        vraw_pool = ctx.enter_context(tc.tile_pool(name="vrawp", bufs=3))
+        do_pool = ctx.enter_context(tc.tile_pool(name="dorawp", bufs=3))
+        raw_pool = ctx.enter_context(tc.tile_pool(name="rawp", bufs=2))
+        work = ctx.enter_context(tc.tile_pool(name="work", bufs=2))
+        one = ctx.enter_context(tc.tile_pool(name="one", bufs=1))
+        dp_pool = ctx.enter_context(tc.psum_pool(name="dp", bufs=6))
+        dk_pool = ctx.enter_context(tc.psum_pool(name="dk", bufs=2))
+
+        offsets = hold.tile([P, B * N // 16], U16, name="offsets")
+        nc.sync.dma_start(offsets[:], offs)
+
+        pool16 = [[hold.tile([P, T, 2], BF16, name=f"pool{g}{u}", align_bytes=64) for u in range(2)] for g in range(G)]
+        windows = [[hold.tile([P, SEG * (b + 1)], F32, name=f"window{b}{h}") for h in range(2)] for b in range(B)]
+        delta_t = hold.tile([P, B, PACK], F32, name="delta_t")
+        minus_delta = hold.tile([P, B, PACK], F32, name="minus_delta")
+
+        def load_v(g, u, pieces):
+            raw = vraw_pool.tile([P, 2, T], F32, name="vraw")
+            src = vT[g * K_PASS : (g + 1) * K_PASS, :].rearrange("(p u e) w -> p u e w", u=2, e=2)
+            n = T // pieces
+            for i in range(pieces):
+                nc.sync.dma_start(raw[:, :, i * n : (i + 1) * n], src[:, u, :, i * n : (i + 1) * n])
+            return raw
+
+        def load_do(b, g):
+            raw = do_pool.tile([P, PACK, NQ], F32, name="doraw")
+            nc.sync.dma_start(raw[:], doT[b, g * K_PASS : (g + 1) * K_PASS, :].rearrange("(p j) q -> p j q", j=PACK))
+            return raw
+
+        def load_p(b):
+            raw = raw_pool.tile([P, PACK, N], F32, name="praw")
+            nc.sync.dma_start(raw[:], p[b].rearrange("(m t) i -> m t i", t=PACK))
+            return raw
+
+        def load_qm(b):
+            raw = raw_pool.tile([P, PACK, D], F32, name="qmraw")
+            nc.sync.dma_start(raw[:], qm[b].rearrange("(m t) d -> m t d", t=PACK))
+            return raw
+
+        def cast_v(b, g, u, shares):
+            for engine, lo, hi in shares:
+                w = slice(b * SEG + lo, b * SEG + hi)
+                move(nc, engine, pool16[g][u][:, w, :], vraw[g, u][:, :, w].rearrange("p e w -> p w e"))
+
+        def gather(b, g, u):
+            words = pool16[g][u][:].rearrange("p w e -> p (w e)").bitcast(U32)[:, 0 : (b + 1) * SEG]
+            if u == 0:
+                pairs[b, g] = work.tile([P, 2, N * 2], BF16, name="pairs", align_bytes=64)
+            nc.vector.tensor_copy(
+                pairs[b, g][:, u, :].bitcast(U32), words.indirect(offsets[:, b * COLS : (b + 1) * COLS])
+            )
+
+        def quantise(x16, name, width, fmt, pieces=1):
+            codes = work.tile([P, width], U32, name=name, align_bytes=64)
+            scales = work.tile([P, width], U8, name=name + "_s", align_bytes=64)
+            n = width // pieces
+            for i in range(pieces):
+                nc.vector.quantize_mx(
+                    out=codes[:, i * n : (i + 1) * n].bitcast(fmt),
+                    scales=scales[:, i * n : (i + 1) * n],
+                    in_=x16[:, i * n * PACK : (i + 1) * n * PACK],
+                )
+            return codes, scales
+
+        def pack_v(b, g):
+            v16 = work.tile([P, N * PACK], BF16, name="v16", align_bytes=64)
+            nc.vector.tensor_copy(
+                v16[:].rearrange("p (n u e) -> p n u e", u=2, e=2),
+                pairs[b, g][:].rearrange("p u (n e) -> p n u e", e=2),
+            )
+            v16s[b, g] = v16
+
+        def cast_do(b, g, shares):
+            do16 = work.tile([P, PACK * NQ], BF16, name="do16", align_bytes=64)
+            dst = do16[:].rearrange("p (t m j) -> p m j t", t=PACK, j=PACK)
+            src = doraw[b, g][:].rearrange("p j (m t) -> p m j t", t=PACK)
+            for engine, lo, hi in shares:
+                move(nc, engine, dst[:, lo:hi], src[:, lo:hi])
+            do16s[b, g] = do16
+
+        def cast_qm(b, shares):
+            qm16 = work.tile([P, D * PACK], BF16, name="qm16", align_bytes=64)
+            dst = qm16[:].rearrange("p (d t) -> p d t", t=PACK)
+            for engine, lo, hi in shares:
+                move(nc, engine, dst[:, lo:hi], qmraw[b][:, :, lo:hi].rearrange("p t d -> p d t"))
+            qm16s[b] = qm16
+
+        def first_product(b):
+            e = one.tile([P, PACK, N], F32, name="e")
+            for t in range(PACK):
+                acc = dp_pool.tile([P, N], F32, name="acc")
+                cols = slice(t * P, (t + 1) * P)
+                for g in range(G):
+                    nc.tensor.matmul_mx(
+                        out=acc[:],
+                        lhsT=doq[b, g][0][:, cols].bitcast(E5M2),
+                        lhsT_scale=doq[b, g][1][:, cols],
+                        rhs=vq[b, g][0][:].bitcast(E4M3),
+                        rhs_scale=vq[b, g][1][:],
+                        start=(g == 0),
+                        stop=(g == G - 1),
+                    )
+                nc.scalar.activation(e[:, t, :], acc[:], IDENT, bias=minus_delta[:, b, t : t + 1])
+            return e
+
+        def weigh(b, e, pieces):
+            ds16 = work.tile([P, N * PACK], BF16, name="ds16", align_bytes=64)
+            dst = ds16[:].rearrange("p (c i t) -> p c t i", t=PACK, i=4)
+            in0 = e[:].rearrange("p t (c i) -> p c t i", i=4)
+            in1 = praw[b][:].rearrange("p t (c i) -> p c t i", i=4)
+            n = N // 4 // pieces
+            for i in range(pieces):
+                c = slice(i * n, (i + 1) * n)
+                nc.vector.tensor_tensor(dst[:, c], in0[:, c], in1[:, c], MUL)
+            return ds16
+
+        def second_product(b, dsq):
+            dks = []
+            for h in range(2):
+                acc = dk_pool.tile([P, N], F32, name="dk")
+                cols = slice(h * P, (h + 1) * P)
+                nc.tensor.matmul_mx(
+                    out=acc[:],
+                    lhsT=qmq[b][0][:, cols].bitcast(E4M3),
+                    lhsT_scale=qmq[b][1][:, cols],
+                    rhs=dsq[0][:].bitcast(E5M2),
+                    rhs_scale=dsq[1][:],
+                    start=True,
+                    stop=True,
+                )
+                dk = work.tile([P, N], F32, name=f"dk_sb{b}")
+                nc.scalar.activation(dk[:], acc[:], COPY)
+                dks.append(dk)
+            return dks
+
+        def scatter(b, h, dk, part, parts):
+            n = N // parts
+            c0 = b * COLS + part * COLS // parts
+            nc.vector.tensor_copy(
+                windows[b][h][:].indirect(offsets[:, c0 : c0 + COLS // parts]), dk[:, part * n : (part + 1) * n]
+            )
+
+        def store(b, h):
+            nc.sync.dma_start(out[h * P : (h + 1) * P, b * SEG : (b + 1) * SEG], windows[b][h][:, b * SEG : (b + 1) * SEG])
+
+        vraw, doraw, praw, qmraw, pairs, v16s, do16s, qm16s, vq, doq, qmq = {}, {}, {}, {}, {}, {}, {}, {}, {}, {}, {}
+
+        vraw[0, 0] = load_v(0, 0, 2)
+        nc.sync.dma_start(delta_t[:], delta.rearrange("b (m t) o -> m b (t o)", t=PACK))
+        vraw[0, 1] = load_v(0, 1, 1)
+        vraw[1, 0] = load_v(1, 0, 1)
+        for b in range(B):
+            for h in range(2):
+                nc.gpsimd.memset(windows[b][h][:, b * SEG : (b + 1) * SEG], 0.0)
+        nc.vector.tensor_scalar(minus_delta[:], delta_t[:], -1.0, None, MUL)
+        for g in range(G):
+            for u in range(2):
+                for b in range(B):
+                    cast_v(b, g, u, share(SEG, 0.3))
+                    gather(b, g, u)
+                if (g, u) == (0, 0):
+                    vraw[1, 1] = load_v(1, 1, 2)
+                    doraw[0, 0] = load_do(0, 0)
+                    doraw[0, 1] = load_do(0, 1)
+                    praw[0] = load_p(0)
+                    qmraw[0] = load_qm(0)
+                    doraw[1, 0] = load_do(1, 0)
+            for b in range(B):
+                pack_v(b, g)
+            for b in range(B):
+                vq[b, g] = quantise(v16s[b, g], f"v{g}", N, E4M3)
+        cast_do(0, 0, share(P, 0.25))
+        doq[0, 0] = quantise(do16s[0, 0], "do0", NQ, E5M2)
+        doraw[1, 1] = load_do(1, 1)
+        qmraw[1] = load_qm(1)
+        praw[1] = load_p(1)
+        cast_do(0, 1, share(P, 0.4))
+        doq[0, 1] = quantise(do16s[0, 1], "do1", NQ, E5M2)
+        e = first_product(0)
+        cast_qm(0, share(D, 0.0))
+        qmq[0] = quantise(qm16s[0], "qm", D, E4M3)
+        ds16 = weigh(0, e, 1)
+        cast_do(1, 0, share(P, 0.25))
+        dsq = quantise(ds16, "ds", N, E5M2)
+        doq[1, 0] = quantise(do16s[1, 0], "do0", NQ, E5M2)
+        dks0 = second_product(0, dsq)
+        cast_do(1, 1, share(P, 0.25))
+        scatter(0, 0, dks0[0], 0, 2)
+        doq[1, 1] = quantise(do16s[1, 1], "do1", NQ, E5M2)
+        scatter(0, 0, dks0[0], 1, 2)
+        store(0, 0)
+        cast_qm(1, share(D, 0.0))
+        qmq[1] = quantise(qm16s[1], "qm", D, E4M3)
+        scatter(0, 1, dks0[1], 0, 2)
+        e = first_product(1)
+        ds16 = weigh(1, e, 2)
+        dsq = quantise(ds16, "ds", N, E5M2, 2)
+        dks = second_product(1, dsq)
+        scatter(0, 1, dks0[1], 1, 2)
+        store(0, 1)
+        for h in range(2):
+            scatter(1, h, dks[h], 0, 1)
+            store(1, h)

@@ -16,6 +16,7 @@ E5M2 = mybir.dt.float8_e5m2_x4
 COPY = mybir.ActivationFunctionType.Copy
 IDENT = mybir.ActivationFunctionType.Identity
 ADD = mybir.AluOpType.add
+SUB = mybir.AluOpType.subtract
 MUL = mybir.AluOpType.mult
 
 P = 128
@@ -46,7 +47,7 @@ def tile_attend_bwd_seg_kernel(tc, doT, vT, p, delta, qm, offs, out):
     nc = tc.nc
     with ExitStack() as ctx:
         hold = ctx.enter_context(tc.tile_pool(name="hold", bufs=1))
-        vraw_pool = ctx.enter_context(tc.tile_pool(name="vrawp", bufs=3))
+        vraw_pool = ctx.enter_context(tc.tile_pool(name="vrawp", bufs=6))
         do_pool = ctx.enter_context(tc.tile_pool(name="dorawp", bufs=3))
         raw_pool = ctx.enter_context(tc.tile_pool(name="rawp", bufs=2))
         work = ctx.enter_context(tc.tile_pool(name="work", bufs=2))
@@ -62,13 +63,13 @@ def tile_attend_bwd_seg_kernel(tc, doT, vT, p, delta, qm, offs, out):
         delta_t = hold.tile([P, B, PACK], F32, name="delta_t")
         minus_delta = hold.tile([P, B, PACK], F32, name="minus_delta")
 
-        def load_v(g, u, pieces):
-            raw = vraw_pool.tile([P, 2, T], F32, name="vraw")
-            src = vT[g * K_PASS : (g + 1) * K_PASS, :].rearrange("(p u e) w -> p u e w", u=2, e=2)
-            n = T // pieces
+        def load_v(b, g, u, pieces=1):
+            raw = vraw_pool.tile([P, 2, SEG], F32, name="vraw")
+            src = vT[g * K_PASS : (g + 1) * K_PASS, b * SEG : (b + 1) * SEG].rearrange("(p u e) w -> p u e w", u=2, e=2)
+            n = SEG // pieces
             for i in range(pieces):
                 nc.sync.dma_start(raw[:, :, i * n : (i + 1) * n], src[:, u, :, i * n : (i + 1) * n])
-            return raw
+            vraw[b, g, u] = raw
 
         def load_do(b, g):
             raw = do_pool.tile([P, PACK, NQ], F32, name="doraw")
@@ -87,8 +88,7 @@ def tile_attend_bwd_seg_kernel(tc, doT, vT, p, delta, qm, offs, out):
 
         def cast_v(b, g, u, shares):
             for engine, lo, hi in shares:
-                w = slice(b * SEG + lo, b * SEG + hi)
-                move(nc, engine, pool16[g][u][:, w, :], vraw[g, u][:, :, w].rearrange("p e w -> p w e"))
+                move(nc, engine, pool16[g][u][:, b * SEG + lo : b * SEG + hi, :], vraw[b, g, u][:, :, lo:hi].rearrange("p e w -> p w e"))
 
         def gather(b, g, u):
             words = pool16[g][u][:].rearrange("p w e -> p (w e)").bitcast(U32)[:, 0 : (b + 1) * SEG]
@@ -151,6 +151,28 @@ def tile_attend_bwd_seg_kernel(tc, doT, vT, p, delta, qm, offs, out):
                 nc.scalar.activation(e[:, t, :], acc[:], IDENT, bias=minus_delta[:, b, t : t + 1])
             return e
 
+        def first_product_v(b):
+            ds_pl = one.tile([P, PACK, N], BF16, name="ds_pl", align_bytes=64)
+            for t in range(PACK):
+                acc = dp_pool.tile([P, N], F32, name="acc")
+                cols = slice(t * P, (t + 1) * P)
+                for g in range(G):
+                    nc.tensor.matmul_mx(
+                        out=acc[:],
+                        lhsT=doq[b, g][0][:, cols].bitcast(E5M2),
+                        lhsT_scale=doq[b, g][1][:, cols],
+                        rhs=vq[b, g][0][:].bitcast(E4M3),
+                        rhs_scale=vq[b, g][1][:],
+                        start=(g == 0),
+                        stop=(g == G - 1),
+                    )
+                nc.vector.scalar_tensor_tensor(
+                    out=ds_pl[:, t, :], in0=acc[:], scalar=delta_t[:, b, t : t + 1], in1=praw[b][:, t, :], op0=SUB, op1=MUL
+                )
+            ds16 = work.tile([P, N * PACK], BF16, name="ds16", align_bytes=64)
+            nc.vector.tensor_copy(ds16[:].rearrange("p (i t) -> p i t", t=PACK), ds_pl[:].rearrange("p t i -> p i t"))
+            return ds16
+
         def weigh(b, e, pieces):
             ds16 = work.tile([P, N * PACK], BF16, name="ds16", align_bytes=64)
             dst = ds16[:].rearrange("p (c i t) -> p c t i", t=PACK, i=4)
@@ -193,52 +215,72 @@ def tile_attend_bwd_seg_kernel(tc, doT, vT, p, delta, qm, offs, out):
 
         vraw, doraw, praw, qmraw, pairs, v16s, do16s, qm16s, vq, doq, qmq = {}, {}, {}, {}, {}, {}, {}, {}, {}, {}, {}
 
-        vraw[0, 0] = load_v(0, 0, 2)
+        def step_do(b, g, gps):
+            cast_do(b, g, share(P, 0.0, gps))
+            doq[b, g] = quantise(do16s[b, g], f"do{g}", NQ, E5M2)
+
+        def step_qm(b, gps):
+            cast_qm(b, share(D, 0.0, gps))
+            qmq[b] = quantise(qm16s[b], "qm", D, E4M3)
+
+        def step_vq(b, g):
+            vq[b, g] = quantise(v16s[b, g], f"v{g}", N, E4M3)
+
+        def step_v(b, g, u):
+            cast_v(b, g, u, share(SEG, 0.0))
+            gather(b, g, u)
+
+        load_v(0, 0, 0, 2)
+        load_v(0, 0, 1)
         nc.sync.dma_start(delta_t[:], delta.rearrange("b (m t) o -> m b (t o)", t=PACK))
-        vraw[0, 1] = load_v(0, 1, 1)
-        vraw[1, 0] = load_v(1, 0, 1)
+        doraw[0, 0] = load_do(0, 0)
+        load_v(0, 1, 0)
+        load_v(0, 1, 1)
+        doraw[0, 1] = load_do(0, 1)
+        load_v(1, 0, 0)
+        praw[0] = load_p(0)
+        load_v(1, 0, 1)
         for b in range(B):
             for h in range(2):
                 nc.gpsimd.memset(windows[b][h][:, b * SEG : (b + 1) * SEG], 0.0)
+        cast_v(0, 0, 0, [("scalar", 0, 256), ("vector", 256, 512)])
+        cast_v(0, 0, 0, [("scalar", 512, 768), ("vector", 768, 1024)])
+        gather(0, 0, 0)
         nc.vector.tensor_scalar(minus_delta[:], delta_t[:], -1.0, None, MUL)
-        for g in range(G):
-            for u in range(2):
-                for b in range(B):
-                    cast_v(b, g, u, share(SEG, 0.3))
-                    gather(b, g, u)
-                if (g, u) == (0, 0):
-                    vraw[1, 1] = load_v(1, 1, 2)
-                    doraw[0, 0] = load_do(0, 0)
-                    doraw[0, 1] = load_do(0, 1)
-                    praw[0] = load_p(0)
-                    qmraw[0] = load_qm(0)
-                    doraw[1, 0] = load_do(1, 0)
-            for b in range(B):
-                pack_v(b, g)
-            for b in range(B):
-                vq[b, g] = quantise(v16s[b, g], f"v{g}", N, E4M3)
-        cast_do(0, 0, share(P, 0.25))
-        doq[0, 0] = quantise(do16s[0, 0], "do0", NQ, E5M2)
+        step_v(0, 0, 1)
+        load_v(1, 1, 0)
+        qmraw[0] = load_qm(0)
+        load_v(1, 1, 1)
+        doraw[1, 0] = load_do(1, 0)
+        pack_v(0, 0)
+        step_do(0, 0, 0.0)
+        step_vq(0, 0)
+        step_v(0, 1, 0)
         doraw[1, 1] = load_do(1, 1)
-        qmraw[1] = load_qm(1)
         praw[1] = load_p(1)
-        cast_do(0, 1, share(P, 0.4))
-        doq[0, 1] = quantise(do16s[0, 1], "do1", NQ, E5M2)
-        e = first_product(0)
-        cast_qm(0, share(D, 0.0))
-        qmq[0] = quantise(qm16s[0], "qm", D, E4M3)
-        ds16 = weigh(0, e, 1)
-        cast_do(1, 0, share(P, 0.25))
+        qmraw[1] = load_qm(1)
+        step_v(0, 1, 1)
+        pack_v(0, 1)
+        step_do(0, 1, 0.0)
+        step_vq(0, 1)
+        step_v(1, 0, 0)
+        ds16 = first_product_v(0)
+        step_v(1, 0, 1)
         dsq = quantise(ds16, "ds", N, E5M2)
-        doq[1, 0] = quantise(do16s[1, 0], "do0", NQ, E5M2)
+        pack_v(1, 0)
+        step_v(1, 1, 0)
+        step_qm(0, 0.0)
+        step_vq(1, 0)
+        step_v(1, 1, 1)
+        pack_v(1, 1)
+        step_do(1, 0, 0.0)
         dks0 = second_product(0, dsq)
-        cast_do(1, 1, share(P, 0.25))
+        step_vq(1, 1)
+        step_do(1, 1, 0.0)
         scatter(0, 0, dks0[0], 0, 2)
-        doq[1, 1] = quantise(do16s[1, 1], "do1", NQ, E5M2)
         scatter(0, 0, dks0[0], 1, 2)
         store(0, 0)
-        cast_qm(1, share(D, 0.0))
-        qmq[1] = quantise(qm16s[1], "qm", D, E4M3)
+        step_qm(1, 0.0)
         scatter(0, 1, dks0[1], 0, 2)
         e = first_product(1)
         ds16 = weigh(1, e, 2)

@@ -169,6 +169,9 @@ def tile_attend_bwd_seg_kernel(tc, doT, vT, p, delta, qm, offs, out):
                 nc.vector.scalar_tensor_tensor(
                     out=ds_pl[:, t, :], in0=acc[:], scalar=delta_t[:, b, t : t + 1], in1=praw[b][:, t, :], op0=SUB, op1=MUL
                 )
+            return ds_pl
+
+        def interleave_v(ds_pl):
             ds16 = work.tile([P, N * PACK], BF16, name="ds16", align_bytes=64)
             nc.vector.tensor_copy(ds16[:].rearrange("p (i t) -> p i t", t=PACK), ds_pl[:].rearrange("p t i -> p i t"))
             return ds16
@@ -184,24 +187,20 @@ def tile_attend_bwd_seg_kernel(tc, doT, vT, p, delta, qm, offs, out):
                 nc.vector.tensor_tensor(dst[:, c], in0[:, c], in1[:, c], MUL)
             return ds16
 
-        def second_product(b, dsq):
-            dks = []
-            for h in range(2):
-                acc = dk_pool.tile([P, N], F32, name="dk")
-                cols = slice(h * P, (h + 1) * P)
-                nc.tensor.matmul_mx(
-                    out=acc[:],
-                    lhsT=qmq[b][0][:, cols].bitcast(E4M3),
-                    lhsT_scale=qmq[b][1][:, cols],
-                    rhs=dsq[0][:].bitcast(E5M2),
-                    rhs_scale=dsq[1][:],
-                    start=True,
-                    stop=True,
-                )
-                dk = work.tile([P, N], F32, name=f"dk_sb{b}")
-                nc.scalar.activation(dk[:], acc[:], COPY)
-                dks.append(dk)
-            return dks
+        def second_product(b, dsq, h, dk):
+            acc = dk_pool.tile([P, N], F32, name="dk")
+            cols = slice(h * P, (h + 1) * P)
+            nc.tensor.matmul_mx(
+                out=acc[:],
+                lhsT=qmq[b][0][:, cols].bitcast(E4M3),
+                lhsT_scale=qmq[b][1][:, cols],
+                rhs=dsq[0][:].bitcast(E5M2),
+                rhs_scale=dsq[1][:],
+                start=True,
+                stop=True,
+            )
+            nc.scalar.activation(dk[:], acc[:], COPY)
+            return dk
 
         def scatter(b, h, dk, part, parts):
             n = N // parts
@@ -215,79 +214,98 @@ def tile_attend_bwd_seg_kernel(tc, doT, vT, p, delta, qm, offs, out):
 
         vraw, doraw, praw, qmraw, pairs, v16s, do16s, qm16s, vq, doq, qmq = {}, {}, {}, {}, {}, {}, {}, {}, {}, {}, {}
 
-        def step_do(b, g, gps):
-            cast_do(b, g, share(P, 0.0, gps))
+        def quant_do(b, g):
             doq[b, g] = quantise(do16s[b, g], f"do{g}", NQ, E5M2)
 
-        def step_qm(b, gps):
-            cast_qm(b, share(D, 0.0, gps))
+        def quant_qm(b):
             qmq[b] = quantise(qm16s[b], "qm", D, E4M3)
 
-        def step_vq(b, g):
+        def quant_v(b, g):
             vq[b, g] = quantise(v16s[b, g], f"v{g}", N, E4M3)
 
-        def step_v(b, g, u):
-            cast_v(b, g, u, share(SEG, 0.0))
-            gather(b, g, u)
+        def part(lo, hi, vec):
+            return [(e_, lo + a, lo + z) for e_, a, z in share(hi - lo, vec)]
 
-        load_v(0, 0, 0, 2)
+        load_v(0, 0, 0)
         load_v(0, 0, 1)
         nc.sync.dma_start(delta_t[:], delta.rearrange("b (m t) o -> m b (t o)", t=PACK))
-        doraw[0, 0] = load_do(0, 0)
-        load_v(0, 1, 0)
-        load_v(0, 1, 1)
-        doraw[0, 1] = load_do(0, 1)
         load_v(1, 0, 0)
-        praw[0] = load_p(0)
         load_v(1, 0, 1)
+        load_v(0, 1, 0, 2)
+        load_v(0, 1, 1)
+        doraw[0, 0] = load_do(0, 0)
+        doraw[0, 1] = load_do(0, 1)
         for b in range(B):
             for h in range(2):
                 nc.gpsimd.memset(windows[b][h][:, b * SEG : (b + 1) * SEG], 0.0)
-        cast_v(0, 0, 0, [("scalar", 0, 256), ("vector", 256, 512)])
-        cast_v(0, 0, 0, [("scalar", 512, 768), ("vector", 768, 1024)])
-        gather(0, 0, 0)
         nc.vector.tensor_scalar(minus_delta[:], delta_t[:], -1.0, None, MUL)
-        step_v(0, 0, 1)
+        cast_v(0, 0, 0, part(0, SEG, 0.25))
+        gather(0, 0, 0)
+        cast_v(0, 0, 1, part(0, SEG, 0.0))
+        gather(0, 0, 1)
         load_v(1, 1, 0)
+        praw[0] = load_p(0)
         qmraw[0] = load_qm(0)
         load_v(1, 1, 1)
         doraw[1, 0] = load_do(1, 0)
+        cast_v(1, 0, 0, part(0, SEG, 0.0))
         pack_v(0, 0)
-        step_do(0, 0, 0.0)
-        step_vq(0, 0)
-        step_v(0, 1, 0)
-        doraw[1, 1] = load_do(1, 1)
-        praw[1] = load_p(1)
-        qmraw[1] = load_qm(1)
-        step_v(0, 1, 1)
-        pack_v(0, 1)
-        step_do(0, 1, 0.0)
-        step_vq(0, 1)
-        step_v(1, 0, 0)
-        ds16 = first_product_v(0)
-        step_v(1, 0, 1)
-        dsq = quantise(ds16, "ds", N, E5M2)
+        quant_v(0, 0)
+        gather(1, 0, 0)
+        cast_v(1, 0, 1, part(0, SEG, 0.0))
+        cast_v(0, 1, 0, part(0, SEG // 2, 0.5))
+        gather(1, 0, 1)
+        cast_v(0, 1, 0, part(SEG // 2, SEG, 0.5))
         pack_v(1, 0)
-        step_v(1, 1, 0)
-        step_qm(0, 0.0)
-        step_vq(1, 0)
-        step_v(1, 1, 1)
+        gather(0, 1, 0)
+        quant_v(1, 0)
+        cast_v(0, 1, 1, part(0, SEG, 0.0))
+        gather(0, 1, 1)
+        cast_do(0, 0, share(P, 0.0))
+        doraw[1, 1] = load_do(1, 1)
+        qmraw[1] = load_qm(1)
+        praw[1] = load_p(1)
+        pack_v(0, 1)
+        quant_v(0, 1)
+        quant_do(0, 0)
+        cast_do(0, 1, share(P, 0.25))
+        quant_do(0, 1)
+        cast_v(1, 1, 0, part(0, SEG, 0.5))
+        gather(1, 1, 0)
+        ds_pl = first_product_v(0)
+        cast_qm(0, share(D, 0.0))
+        ds16 = interleave_v(ds_pl)
+        quant_qm(0)
+        dsq = quantise(ds16, "ds", N, E5M2)
+        cast_v(1, 1, 1, part(0, SEG, 0.0))
+        gather(1, 1, 1)
+        cast_do(1, 0, share(P, 0.25))
         pack_v(1, 1)
-        step_do(1, 0, 0.0)
-        dks0 = second_product(0, dsq)
-        step_vq(1, 1)
-        step_do(1, 1, 0.0)
-        scatter(0, 0, dks0[0], 0, 2)
-        scatter(0, 0, dks0[0], 1, 2)
-        store(0, 0)
-        step_qm(1, 0.0)
-        scatter(0, 1, dks0[1], 0, 2)
+        quant_v(1, 1)
+        cast_do(1, 1, share(P, 0.5))
+        quant_do(1, 0)
+        dk00 = work.tile([P, N], F32, name="do16", align_bytes=64)
+        second_product(0, dsq, 0, dk00)
+        scatter(0, 0, dk00, 0, 2)
+        quant_do(1, 1)
+        cast_qm(1, share(D, 0.0))
         e = first_product(1)
+        quant_qm(1)
         ds16 = weigh(1, e, 2)
-        dsq = quantise(ds16, "ds", N, E5M2, 2)
-        dks = second_product(1, dsq)
-        scatter(0, 1, dks0[1], 1, 2)
+        dk01 = work.tile([P, N], F32, name="do16", align_bytes=64)
+        second_product(0, dsq, 1, dk01)
+        scatter(0, 0, dk00, 1, 2)
+        store(0, 0)
+        scatter(0, 1, dk01, 0, 2)
+        dsq1 = quantise(ds16, "ds", N, E5M2, 2)
+        scatter(0, 1, dk01, 1, 2)
         store(0, 1)
+        dks = []
         for h in range(2):
-            scatter(1, h, dks[h], 0, 1)
+            dk = work.tile([P, N], F32, name="dk_sb")
+            dks.append(second_product(1, dsq1, h, dk))
+        scatter(1, 0, dks[0], 0, 2)
+        scatter(1, 1, dks[1], 0, 2)
+        for h in range(2):
+            scatter(1, h, dks[h], 1, 2)
             store(1, h)

@@ -3,6 +3,7 @@ from contextlib import ExitStack
 import concourse.mybir as mybir
 
 B, N, T, D, DV, NQ = 2, 512, 2048, 256, 1024, 512
+
 FLOPS = 2 * B * NQ * N * (DV + D)
 BYTES = 4 * (B * DV * NQ + DV * B * N + B * NQ * N + B * NQ + B * NQ * D + D * T) + 2 * 128 * (B * N // 16)
 
@@ -14,88 +15,112 @@ U8 = mybir.dt.uint8
 E4M3 = mybir.dt.float8_e4m3fn_x4
 E5M2 = mybir.dt.float8_e5m2_x4
 COPY = mybir.ActivationFunctionType.Copy
-IDENT = mybir.ActivationFunctionType.Identity
-ADD = mybir.AluOpType.add
-SUB = mybir.AluOpType.subtract
-MUL = mybir.AluOpType.mult
+IDENTITY = mybir.ActivationFunctionType.Identity
+SUBTRACT = mybir.AluOpType.subtract
+MULTIPLY = mybir.AluOpType.mult
 
 P = 128
-PACK = 4
-K_PASS = P * PACK
+PLACES = 4
+PASS = P * PLACES
+PASSES = DV // PASS
 SEG = T // B
-G = DV // K_PASS
-COLS = N // 16
-
-
-def move(nc, engine, out, in_):
-    if engine == "scalar":
-        nc.scalar.activation(out, in_, COPY)
-    elif engine == "vector":
-        nc.vector.tensor_copy(out, in_)
-    else:
-        nc.gpsimd.tensor_scalar(out, in_, 1.0, 0.0, MUL, ADD)
-
-
-def share(width, vec, gps=0.0):
-    v = int(width * vec) // 8 * 8
-    g = int(width * gps) // 8 * 8
-    s = width - v - g
-    return [x for x in [("scalar", 0, s), ("vector", s, s + v), ("gpsimd", s + v, width)] if x[1] < x[2]]
+LIST_COLS = N // 16
+RUN = 4
 
 
 def tile_attend_bwd_seg_kernel(tc, doT, vT, p, delta, qm, offs, out):
     nc = tc.nc
     with ExitStack() as ctx:
         hold = ctx.enter_context(tc.tile_pool(name="hold", bufs=1))
-        vraw_pool = ctx.enter_context(tc.tile_pool(name="vrawp", bufs=6))
-        do_pool = ctx.enter_context(tc.tile_pool(name="dorawp", bufs=3))
-        raw_pool = ctx.enter_context(tc.tile_pool(name="rawp", bufs=2))
+        v_raw_pool = ctx.enter_context(tc.tile_pool(name="v_raw", bufs=6))
+        do_raw_pool = ctx.enter_context(tc.tile_pool(name="do_raw", bufs=3))
+        raw_pool = ctx.enter_context(tc.tile_pool(name="raw", bufs=2))
         work = ctx.enter_context(tc.tile_pool(name="work", bufs=2))
-        one = ctx.enter_context(tc.tile_pool(name="one", bufs=1))
+        single = ctx.enter_context(tc.tile_pool(name="single", bufs=1))
         dp_pool = ctx.enter_context(tc.psum_pool(name="dp", bufs=6))
         dk_pool = ctx.enter_context(tc.psum_pool(name="dk", bufs=2))
 
         offsets = hold.tile([P, B * N // 16], U16, name="offsets")
         nc.sync.dma_start(offsets[:], offs)
 
-        pool16 = [[hold.tile([P, T, 2], BF16, name=f"pool{g}{u}", align_bytes=64) for u in range(2)] for g in range(G)]
+        pool16 = [
+            [hold.tile([P, T, 2], BF16, name=f"pool{g}{u}", align_bytes=64) for u in range(2)] for g in range(PASSES)
+        ]
         windows = [[hold.tile([P, SEG * (b + 1)], F32, name=f"window{b}{h}") for h in range(2)] for b in range(B)]
-        delta_t = hold.tile([P, B, PACK], F32, name="delta_t")
-        minus_delta = hold.tile([P, B, PACK], F32, name="minus_delta")
+        delta_t = hold.tile([P, B, PLACES], F32, name="delta_t")
+        minus_delta = hold.tile([P, B, PLACES], F32, name="minus_delta")
+
+        v_raw, do_raw, p_raw, qm_raw = {}, {}, {}, {}
+        pairs, v16, do16, qm16 = {}, {}, {}, {}
+        v_mx, do_mx, qm_mx = {}, {}, {}
+
 
         def load_v(b, g, u, pieces=1):
-            raw = vraw_pool.tile([P, 2, SEG], F32, name="vraw")
-            src = vT[g * K_PASS : (g + 1) * K_PASS, b * SEG : (b + 1) * SEG].rearrange("(p u e) w -> p u e w", u=2, e=2)
-            n = SEG // pieces
+            tile = v_raw_pool.tile([P, 2, SEG], F32, name="vraw")
+            rows = vT[g * PASS : (g + 1) * PASS, b * SEG : (b + 1) * SEG].rearrange("(p u e) w -> p u e w", u=2, e=2)
+            width = SEG // pieces
             for i in range(pieces):
-                nc.sync.dma_start(raw[:, :, i * n : (i + 1) * n], src[:, u, :, i * n : (i + 1) * n])
-            vraw[b, g, u] = raw
+                w = slice(i * width, (i + 1) * width)
+                nc.sync.dma_start(tile[:, :, w], rows[:, u, :, w])
+            v_raw[b, g, u] = tile
 
         def load_do(b, g):
-            raw = do_pool.tile([P, PACK, NQ], F32, name="doraw")
-            nc.sync.dma_start(raw[:], doT[b, g * K_PASS : (g + 1) * K_PASS, :].rearrange("(p j) q -> p j q", j=PACK))
-            return raw
+            tile = do_raw_pool.tile([P, PLACES, NQ], F32, name="doraw")
+            nc.sync.dma_start(tile[:], doT[b, g * PASS : (g + 1) * PASS, :].rearrange("(p j) q -> p j q", j=PLACES))
+            do_raw[b, g] = tile
 
         def load_p(b):
-            raw = raw_pool.tile([P, PACK, N], F32, name="praw")
-            nc.sync.dma_start(raw[:], p[b].rearrange("(m t) i -> m t i", t=PACK))
-            return raw
+            tile = raw_pool.tile([P, PLACES, N], F32, name="praw")
+            nc.sync.dma_start(tile[:], p[b].rearrange("(m t) i -> m t i", t=PLACES))
+            p_raw[b] = tile
 
         def load_qm(b):
-            raw = raw_pool.tile([P, PACK, D], F32, name="qmraw")
-            nc.sync.dma_start(raw[:], qm[b].rearrange("(m t) d -> m t d", t=PACK))
-            return raw
+            tile = raw_pool.tile([P, PLACES, D], F32, name="qmraw")
+            nc.sync.dma_start(tile[:], qm[b].rearrange("(m t) d -> m t d", t=PLACES))
+            qm_raw[b] = tile
 
-        def cast_v(b, g, u, shares):
-            for engine, lo, hi in shares:
-                move(nc, engine, pool16[g][u][:, b * SEG + lo : b * SEG + hi, :], vraw[b, g, u][:, :, lo:hi].rearrange("p e w -> p w e"))
+
+        def round_split(dst, src, lo, hi, vector_cols):
+            cut = hi - vector_cols
+            nc.scalar.activation(dst[:, lo:cut], src[:, lo:cut], COPY)
+            if vector_cols:
+                nc.vector.tensor_copy(dst[:, cut:hi], src[:, cut:hi])
+
+        def round_v(b, g, u, vector_cols=0, lo=0, hi=SEG):
+            dst = pool16[g][u][:, b * SEG : (b + 1) * SEG, :]
+            round_split(dst, v_raw[b, g, u][:].rearrange("p e w -> p w e"), lo, hi, vector_cols)
 
         def gather(b, g, u):
-            words = pool16[g][u][:].rearrange("p w e -> p (w e)").bitcast(U32)[:, 0 : (b + 1) * SEG]
             if u == 0:
                 pairs[b, g] = work.tile([P, 2, N * 2], BF16, name="pairs", align_bytes=64)
+            words = pool16[g][u][:].rearrange("p w e -> p (w e)").bitcast(U32)[:, 0 : (b + 1) * SEG]
             nc.vector.tensor_copy(
-                pairs[b, g][:, u, :].bitcast(U32), words.indirect(offsets[:, b * COLS : (b + 1) * COLS])
+                pairs[b, g][:, u, :].bitcast(U32), words.indirect(offsets[:, b * LIST_COLS : (b + 1) * LIST_COLS])
+            )
+
+        def pack_v(b, g):
+            v16[b, g] = work.tile([P, N * PLACES], BF16, name="v16", align_bytes=64)
+            nc.vector.tensor_copy(
+                v16[b, g][:].rearrange("p (i u e) -> p i u e", u=2, e=2),
+                pairs[b, g][:].rearrange("p u (i e) -> p i u e", e=2),
+            )
+
+        def round_do(b, g, vector_cols=0):
+            do16[b, g] = work.tile([P, NQ * PLACES], BF16, name="do16", align_bytes=64)
+            round_split(
+                do16[b, g][:].rearrange("p (t m j) -> p m j t", t=PLACES, j=PLACES),
+                do_raw[b, g][:].rearrange("p j (m t) -> p m j t", t=PLACES),
+                0,
+                P,
+                vector_cols,
+            )
+
+        def round_qm(b):
+            qm16[b] = work.tile([P, D * PLACES], BF16, name="qm16", align_bytes=64)
+            nc.scalar.activation(
+                qm16[b][:].rearrange("p (c d t) -> p c t d", t=PLACES, d=RUN),
+                qm_raw[b][:].rearrange("p t (c d) -> p c t d", d=RUN),
+                COPY,
             )
 
         def quantise(x16, name, width, fmt, pieces=1):
@@ -103,209 +128,189 @@ def tile_attend_bwd_seg_kernel(tc, doT, vT, p, delta, qm, offs, out):
             scales = work.tile([P, width], U8, name=name + "_s", align_bytes=64)
             n = width // pieces
             for i in range(pieces):
+                cols = slice(i * n, (i + 1) * n)
                 nc.vector.quantize_mx(
-                    out=codes[:, i * n : (i + 1) * n].bitcast(fmt),
-                    scales=scales[:, i * n : (i + 1) * n],
-                    in_=x16[:, i * n * PACK : (i + 1) * n * PACK],
+                    out=codes[:, cols].bitcast(fmt),
+                    scales=scales[:, cols],
+                    in_=x16[:, i * n * PLACES : (i + 1) * n * PLACES],
                 )
             return codes, scales
 
-        def pack_v(b, g):
-            v16 = work.tile([P, N * PACK], BF16, name="v16", align_bytes=64)
-            nc.vector.tensor_copy(
-                v16[:].rearrange("p (n u e) -> p n u e", u=2, e=2),
-                pairs[b, g][:].rearrange("p u (n e) -> p n u e", e=2),
-            )
-            v16s[b, g] = v16
+        def quantise_v(b, g):
+            v_mx[b, g] = quantise(v16[b, g], f"v{g}", N, E4M3)
 
-        def cast_do(b, g, shares):
-            do16 = work.tile([P, PACK * NQ], BF16, name="do16", align_bytes=64)
-            dst = do16[:].rearrange("p (t m j) -> p m j t", t=PACK, j=PACK)
-            src = doraw[b, g][:].rearrange("p j (m t) -> p m j t", t=PACK)
-            for engine, lo, hi in shares:
-                move(nc, engine, dst[:, lo:hi], src[:, lo:hi])
-            do16s[b, g] = do16
+        def quantise_do(b, g):
+            do_mx[b, g] = quantise(do16[b, g], f"do{g}", NQ, E5M2)
 
-        def cast_qm(b, shares):
-            qm16 = work.tile([P, D * PACK], BF16, name="qm16", align_bytes=64)
-            dst = qm16[:].rearrange("p (d t) -> p d t", t=PACK)
-            for engine, lo, hi in shares:
-                move(nc, engine, dst[:, lo:hi], qmraw[b][:, :, lo:hi].rearrange("p t d -> p d t"))
-            qm16s[b] = qm16
+        def quantise_qm(b):
+            qm_mx[b] = quantise(qm16[b], "qm", D, E4M3)
 
-        def first_product(b):
-            e = one.tile([P, PACK, N], F32, name="e")
-            for t in range(PACK):
-                acc = dp_pool.tile([P, N], F32, name="acc")
-                cols = slice(t * P, (t + 1) * P)
-                for g in range(G):
-                    nc.tensor.matmul_mx(
-                        out=acc[:],
-                        lhsT=doq[b, g][0][:, cols].bitcast(E5M2),
-                        lhsT_scale=doq[b, g][1][:, cols],
-                        rhs=vq[b, g][0][:].bitcast(E4M3),
-                        rhs_scale=vq[b, g][1][:],
-                        start=(g == 0),
-                        stop=(g == G - 1),
-                    )
-                nc.scalar.activation(e[:, t, :], acc[:], IDENT, bias=minus_delta[:, b, t : t + 1])
-            return e
 
-        def first_product_v(b):
-            ds_pl = one.tile([P, PACK, N], BF16, name="ds_pl", align_bytes=64)
-            for t in range(PACK):
-                acc = dp_pool.tile([P, N], F32, name="acc")
-                cols = slice(t * P, (t + 1) * P)
-                for g in range(G):
-                    nc.tensor.matmul_mx(
-                        out=acc[:],
-                        lhsT=doq[b, g][0][:, cols].bitcast(E5M2),
-                        lhsT_scale=doq[b, g][1][:, cols],
-                        rhs=vq[b, g][0][:].bitcast(E4M3),
-                        rhs_scale=vq[b, g][1][:],
-                        start=(g == 0),
-                        stop=(g == G - 1),
-                    )
-                nc.vector.scalar_tensor_tensor(
-                    out=ds_pl[:, t, :], in0=acc[:], scalar=delta_t[:, b, t : t + 1], in1=praw[b][:, t, :], op0=SUB, op1=MUL
+        def dp_tile(b, t):
+            dp = dp_pool.tile([P, N], F32, name="dp")
+            cols = slice(t * P, (t + 1) * P)
+            for g in range(PASSES):
+                do_codes, do_scales = do_mx[b, g]
+                v_codes, v_scales = v_mx[b, g]
+                nc.tensor.matmul_mx(
+                    out=dp[:],
+                    lhsT=do_codes[:, cols].bitcast(E5M2),
+                    lhsT_scale=do_scales[:, cols],
+                    rhs=v_codes[:].bitcast(E4M3),
+                    rhs_scale=v_scales[:],
+                    start=(g == 0),
+                    stop=(g == PASSES - 1),
                 )
-            return ds_pl
+            return dp
 
-        def interleave_v(ds_pl):
-            ds16 = work.tile([P, N * PACK], BF16, name="ds16", align_bytes=64)
-            nc.vector.tensor_copy(ds16[:].rearrange("p (i t) -> p i t", t=PACK), ds_pl[:].rearrange("p t i -> p i t"))
+        def ds_from_psum(b):
+            ds = single.tile([P, PLACES, N], BF16, name="ds_rows", align_bytes=64)
+            for t in range(PLACES):
+                nc.vector.scalar_tensor_tensor(
+                    out=ds[:, t, :],
+                    in0=dp_tile(b, t)[:],
+                    scalar=delta_t[:, b, t : t + 1],
+                    in1=p_raw[b][:, t, :],
+                    op0=SUBTRACT,
+                    op1=MULTIPLY,
+                )
+            return ds
+
+        def interleave(ds):
+            ds16 = work.tile([P, N * PLACES], BF16, name="ds16", align_bytes=64)
+            nc.vector.tensor_copy(
+                ds16[:].rearrange("p (c i t) -> p c t i", t=PLACES, i=RUN), ds[:].rearrange("p t (c i) -> p c t i", i=RUN)
+            )
             return ds16
 
-        def weigh(b, e, pieces):
-            ds16 = work.tile([P, N * PACK], BF16, name="ds16", align_bytes=64)
-            dst = ds16[:].rearrange("p (c i t) -> p c t i", t=PACK, i=4)
-            in0 = e[:].rearrange("p t (c i) -> p c t i", i=4)
-            in1 = praw[b][:].rearrange("p t (c i) -> p c t i", i=4)
-            n = N // 4 // pieces
+        def dp_minus_delta(b):
+            diff = single.tile([P, PLACES, N], F32, name="diff")
+            for t in range(PLACES):
+                nc.scalar.activation(diff[:, t, :], dp_tile(b, t)[:], IDENTITY, bias=minus_delta[:, b, t : t + 1])
+            return diff
+
+        def weigh(b, diff, pieces):
+            ds16 = work.tile([P, N * PLACES], BF16, name="ds16", align_bytes=64)
+            dst = ds16[:].rearrange("p (c i t) -> p c t i", t=PLACES, i=RUN)
+            in0 = diff[:].rearrange("p t (c i) -> p c t i", i=RUN)
+            in1 = p_raw[b][:].rearrange("p t (c i) -> p c t i", i=RUN)
+            n = N // RUN // pieces
             for i in range(pieces):
-                c = slice(i * n, (i + 1) * n)
-                nc.vector.tensor_tensor(dst[:, c], in0[:, c], in1[:, c], MUL)
+                runs = slice(i * n, (i + 1) * n)
+                nc.vector.tensor_tensor(dst[:, runs], in0[:, runs], in1[:, runs], MULTIPLY)
             return ds16
 
-        def second_product(b, dsq, h, dk):
-            acc = dk_pool.tile([P, N], F32, name="dk")
+        def second_product(b, ds_mx, h, staged):
+            dk = dk_pool.tile([P, N], F32, name="dk")
             cols = slice(h * P, (h + 1) * P)
             nc.tensor.matmul_mx(
-                out=acc[:],
-                lhsT=qmq[b][0][:, cols].bitcast(E4M3),
-                lhsT_scale=qmq[b][1][:, cols],
-                rhs=dsq[0][:].bitcast(E5M2),
-                rhs_scale=dsq[1][:],
+                out=dk[:],
+                lhsT=qm_mx[b][0][:, cols].bitcast(E4M3),
+                lhsT_scale=qm_mx[b][1][:, cols],
+                rhs=ds_mx[0][:].bitcast(E5M2),
+                rhs_scale=ds_mx[1][:],
                 start=True,
                 stop=True,
             )
-            nc.scalar.activation(dk[:], acc[:], COPY)
-            return dk
+            nc.scalar.activation(staged[:], dk[:], COPY)
 
-        def scatter(b, h, dk, part, parts):
-            n = N // parts
-            c0 = b * COLS + part * COLS // parts
+        def scatter(b, h, staged, piece=0, pieces=1):
+            n = N // pieces
+            first = b * LIST_COLS + piece * LIST_COLS // pieces
             nc.vector.tensor_copy(
-                windows[b][h][:].indirect(offsets[:, c0 : c0 + COLS // parts]), dk[:, part * n : (part + 1) * n]
+                windows[b][h][:].indirect(offsets[:, first : first + LIST_COLS // pieces]),
+                staged[:, piece * n : (piece + 1) * n],
             )
 
         def store(b, h):
-            nc.sync.dma_start(out[h * P : (h + 1) * P, b * SEG : (b + 1) * SEG], windows[b][h][:, b * SEG : (b + 1) * SEG])
+            cols = slice(b * SEG, (b + 1) * SEG)
+            nc.sync.dma_start(out[h * P : (h + 1) * P, cols], windows[b][h][:, cols])
 
-        vraw, doraw, praw, qmraw, pairs, v16s, do16s, qm16s, vq, doq, qmq = {}, {}, {}, {}, {}, {}, {}, {}, {}, {}, {}
-
-        def quant_do(b, g):
-            doq[b, g] = quantise(do16s[b, g], f"do{g}", NQ, E5M2)
-
-        def quant_qm(b):
-            qmq[b] = quantise(qm16s[b], "qm", D, E4M3)
-
-        def quant_v(b, g):
-            vq[b, g] = quantise(v16s[b, g], f"v{g}", N, E4M3)
-
-        def part(lo, hi, vec):
-            return [(e_, lo + a, lo + z) for e_, a, z in share(hi - lo, vec)]
 
         load_v(0, 0, 0)
         load_v(0, 0, 1)
-        nc.sync.dma_start(delta_t[:], delta.rearrange("b (m t) o -> m b (t o)", t=PACK))
+        nc.sync.dma_start(delta_t[:], delta.rearrange("b (m t) o -> m b (t o)", t=PLACES))
         load_v(1, 0, 0)
         load_v(1, 0, 1)
-        load_v(0, 1, 0, 2)
+        load_v(0, 1, 0, pieces=2)
         load_v(0, 1, 1)
-        doraw[0, 0] = load_do(0, 0)
-        doraw[0, 1] = load_do(0, 1)
+        load_do(0, 0)
+        load_do(0, 1)
         for b in range(B):
             for h in range(2):
                 nc.gpsimd.memset(windows[b][h][:, b * SEG : (b + 1) * SEG], 0.0)
-        nc.vector.tensor_scalar(minus_delta[:], delta_t[:], -1.0, None, MUL)
-        cast_v(0, 0, 0, part(0, SEG, 0.25))
+        nc.vector.tensor_scalar(minus_delta[:], delta_t[:], -1.0, None, MULTIPLY)
+
+        round_v(0, 0, 0, vector_cols=SEG // 4)
         gather(0, 0, 0)
-        cast_v(0, 0, 1, part(0, SEG, 0.0))
+        round_v(0, 0, 1)
         gather(0, 0, 1)
         load_v(1, 1, 0)
-        praw[0] = load_p(0)
-        qmraw[0] = load_qm(0)
+        load_p(0)
         load_v(1, 1, 1)
-        doraw[1, 0] = load_do(1, 0)
-        cast_v(1, 0, 0, part(0, SEG, 0.0))
+        load_qm(0)
+        load_do(1, 0)
+        round_v(1, 0, 0)
         pack_v(0, 0)
-        quant_v(0, 0)
+        quantise_v(0, 0)
         gather(1, 0, 0)
-        cast_v(1, 0, 1, part(0, SEG, 0.0))
-        cast_v(0, 1, 0, part(0, SEG // 2, 0.5))
+        round_v(1, 0, 1)
+        round_v(0, 1, 0, vector_cols=SEG // 4, lo=0, hi=SEG // 2)
         gather(1, 0, 1)
-        cast_v(0, 1, 0, part(SEG // 2, SEG, 0.5))
+        round_v(0, 1, 0, vector_cols=SEG // 4, lo=SEG // 2, hi=SEG)
         pack_v(1, 0)
         gather(0, 1, 0)
-        quant_v(1, 0)
-        cast_v(0, 1, 1, part(0, SEG, 0.0))
+        quantise_v(1, 0)
+        round_v(0, 1, 1)
         gather(0, 1, 1)
-        cast_do(0, 0, share(P, 0.0))
-        doraw[1, 1] = load_do(1, 1)
-        qmraw[1] = load_qm(1)
-        praw[1] = load_p(1)
+        round_do(0, 0)
+        load_do(1, 1)
+        load_qm(1)
+        load_p(1)
         pack_v(0, 1)
-        quant_v(0, 1)
-        quant_do(0, 0)
-        cast_do(0, 1, share(P, 0.25))
-        quant_do(0, 1)
-        cast_v(1, 1, 0, part(0, SEG, 0.5))
+        quantise_v(0, 1)
+        quantise_do(0, 0)
+        round_do(0, 1, vector_cols=P // 4)
+        quantise_do(0, 1)
+
+        round_v(1, 1, 0, vector_cols=SEG // 2)
         gather(1, 1, 0)
-        ds_pl = first_product_v(0)
-        cast_qm(0, share(D, 0.0))
-        ds16 = interleave_v(ds_pl)
-        quant_qm(0)
-        dsq = quantise(ds16, "ds", N, E5M2)
-        cast_v(1, 1, 1, part(0, SEG, 0.0))
+        ds_rows = ds_from_psum(0)
+        round_qm(0)
+        ds16 = interleave(ds_rows)
+        quantise_qm(0)
+        ds_mx0 = quantise(ds16, "ds", N, E5M2)
+        round_v(1, 1, 1)
         gather(1, 1, 1)
-        cast_do(1, 0, share(P, 0.25))
+        round_do(1, 0, vector_cols=P // 4)
         pack_v(1, 1)
-        quant_v(1, 1)
-        cast_do(1, 1, share(P, 0.5))
-        quant_do(1, 0)
-        dk00 = work.tile([P, N], F32, name="do16", align_bytes=64)
-        second_product(0, dsq, 0, dk00)
-        scatter(0, 0, dk00, 0, 2)
-        quant_do(1, 1)
-        cast_qm(1, share(D, 0.0))
-        e = first_product(1)
-        quant_qm(1)
-        ds16 = weigh(1, e, 2)
-        dk01 = work.tile([P, N], F32, name="do16", align_bytes=64)
-        second_product(0, dsq, 1, dk01)
-        scatter(0, 0, dk00, 1, 2)
+        quantise_v(1, 1)
+        round_do(1, 1, vector_cols=P // 2)
+        quantise_do(1, 0)
+
+        staged00 = work.tile([P, N], F32, name="do16", align_bytes=64)
+        second_product(0, ds_mx0, 0, staged00)
+        scatter(0, 0, staged00, piece=0, pieces=2)
+        quantise_do(1, 1)
+
+        round_qm(1)
+        diff = dp_minus_delta(1)
+        quantise_qm(1)
+        ds16 = weigh(1, diff, pieces=2)
+        staged01 = work.tile([P, N], F32, name="do16", align_bytes=64)
+        second_product(0, ds_mx0, 1, staged01)
+        scatter(0, 0, staged00, piece=1, pieces=2)
         store(0, 0)
-        scatter(0, 1, dk01, 0, 2)
-        dsq1 = quantise(ds16, "ds", N, E5M2, 2)
-        scatter(0, 1, dk01, 1, 2)
+        scatter(0, 1, staged01, piece=0, pieces=2)
+        ds_mx1 = quantise(ds16, "ds", N, E5M2, pieces=2)
+        scatter(0, 1, staged01, piece=1, pieces=2)
         store(0, 1)
-        dks = []
+
+        staged1 = []
         for h in range(2):
-            dk = work.tile([P, N], F32, name="dk_sb")
-            dks.append(second_product(1, dsq1, h, dk))
-        scatter(1, 0, dks[0], 0, 2)
-        scatter(1, 1, dks[1], 0, 2)
+            staged = work.tile([P, N], F32, name="staged")
+            second_product(1, ds_mx1, h, staged)
+            staged1.append(staged)
         for h in range(2):
-            scatter(1, h, dks[h], 1, 2)
+            scatter(1, h, staged1[h])
             store(1, h)

from contextlib import ExitStack

import concourse.mybir as mybir

B, N, T, D, DV, NQ = 2, 512, 2048, 256, 1024, 512

FLOPS = 2 * B * NQ * N * (DV + D)
BYTES = 4 * (B * DV * NQ + DV * B * N + B * NQ * N + B * NQ + B * NQ * D + D * T) + 2 * 128 * (B * N // 16)

F32 = mybir.dt.float32
BF16 = mybir.dt.bfloat16
U32 = mybir.dt.uint32
U16 = mybir.dt.uint16
U8 = mybir.dt.uint8
E4M3 = mybir.dt.float8_e4m3fn_x4
E5M2 = mybir.dt.float8_e5m2_x4
COPY = mybir.ActivationFunctionType.Copy
IDENTITY = mybir.ActivationFunctionType.Identity
SUBTRACT = mybir.AluOpType.subtract
MULTIPLY = mybir.AluOpType.mult

P = 128
PLACES = 4
PASS = P * PLACES
PASSES = DV // PASS
SEG = T // B
LIST_COLS = N // 16
RUN = 4


def tile_attend_bwd_seg_kernel(tc, doT, vT, p, delta, qm, offs, out):
    nc = tc.nc
    with ExitStack() as ctx:
        hold = ctx.enter_context(tc.tile_pool(name="hold", bufs=1))
        v_raw_pool = ctx.enter_context(tc.tile_pool(name="v_raw", bufs=6))
        do_raw_pool = ctx.enter_context(tc.tile_pool(name="do_raw", bufs=3))
        raw_pool = ctx.enter_context(tc.tile_pool(name="raw", bufs=2))
        work = ctx.enter_context(tc.tile_pool(name="work", bufs=2))
        single = ctx.enter_context(tc.tile_pool(name="single", bufs=1))
        dp_pool = ctx.enter_context(tc.psum_pool(name="dp", bufs=6))
        dk_pool = ctx.enter_context(tc.psum_pool(name="dk", bufs=2))

        offsets = hold.tile([P, B * N // 16], U16, name="offsets")
        nc.sync.dma_start(offsets[:], offs)

        pool16 = [
            [hold.tile([P, T, 2], BF16, name=f"pool{g}{u}", align_bytes=64) for u in range(2)] for g in range(PASSES)
        ]
        windows = [[hold.tile([P, SEG * (b + 1)], F32, name=f"window{b}{h}") for h in range(2)] for b in range(B)]
        delta_t = hold.tile([P, B, PLACES], F32, name="delta_t")
        minus_delta = hold.tile([P, B, PLACES], F32, name="minus_delta")

        v_raw, do_raw, p_raw, qm_raw = {}, {}, {}, {}
        pairs, v16, do16, qm16 = {}, {}, {}, {}
        v_mx, do_mx, qm_mx = {}, {}, {}


        def load_v(b, g, u, pieces=1):
            tile = v_raw_pool.tile([P, 2, SEG], F32, name="vraw")
            rows = vT[g * PASS : (g + 1) * PASS, b * SEG : (b + 1) * SEG].rearrange("(p u e) w -> p u e w", u=2, e=2)
            width = SEG // pieces
            for i in range(pieces):
                w = slice(i * width, (i + 1) * width)
                nc.sync.dma_start(tile[:, :, w], rows[:, u, :, w])
            v_raw[b, g, u] = tile

        def load_do(b, g):
            tile = do_raw_pool.tile([P, PLACES, NQ], F32, name="doraw")
            nc.sync.dma_start(tile[:], doT[b, g * PASS : (g + 1) * PASS, :].rearrange("(p j) q -> p j q", j=PLACES))
            do_raw[b, g] = tile

        def load_p(b):
            tile = raw_pool.tile([P, PLACES, N], F32, name="praw")
            nc.sync.dma_start(tile[:], p[b].rearrange("(m t) i -> m t i", t=PLACES))
            p_raw[b] = tile

        def load_qm(b):
            tile = raw_pool.tile([P, PLACES, D], F32, name="qmraw")
            nc.sync.dma_start(tile[:], qm[b].rearrange("(m t) d -> m t d", t=PLACES))
            qm_raw[b] = tile


        def round_split(dst, src, lo, hi, vector_cols):
            cut = hi - vector_cols
            nc.scalar.activation(dst[:, lo:cut], src[:, lo:cut], COPY)
            if vector_cols:
                nc.vector.tensor_copy(dst[:, cut:hi], src[:, cut:hi])

        def round_v(b, g, u, vector_cols=0, lo=0, hi=SEG):
            dst = pool16[g][u][:, b * SEG : (b + 1) * SEG, :]
            round_split(dst, v_raw[b, g, u][:].rearrange("p e w -> p w e"), lo, hi, vector_cols)

        def gather(b, g, u):
            if u == 0:
                pairs[b, g] = work.tile([P, 2, N * 2], BF16, name="pairs", align_bytes=64)
            words = pool16[g][u][:].rearrange("p w e -> p (w e)").bitcast(U32)[:, 0 : (b + 1) * SEG]
            nc.vector.tensor_copy(
                pairs[b, g][:, u, :].bitcast(U32), words.indirect(offsets[:, b * LIST_COLS : (b + 1) * LIST_COLS])
            )

        def pack_v(b, g):
            v16[b, g] = work.tile([P, N * PLACES], BF16, name="v16", align_bytes=64)
            nc.vector.tensor_copy(
                v16[b, g][:].rearrange("p (i u e) -> p i u e", u=2, e=2),
                pairs[b, g][:].rearrange("p u (i e) -> p i u e", e=2),
            )

        def round_do(b, g, vector_cols=0):
            do16[b, g] = work.tile([P, NQ * PLACES], BF16, name="do16", align_bytes=64)
            round_split(
                do16[b, g][:].rearrange("p (t m j) -> p m j t", t=PLACES, j=PLACES),
                do_raw[b, g][:].rearrange("p j (m t) -> p m j t", t=PLACES),
                0,
                P,
                vector_cols,
            )

        def round_qm(b):
            qm16[b] = work.tile([P, D * PLACES], BF16, name="qm16", align_bytes=64)
            nc.scalar.activation(
                qm16[b][:].rearrange("p (c d t) -> p c t d", t=PLACES, d=RUN),
                qm_raw[b][:].rearrange("p t (c d) -> p c t d", d=RUN),
                COPY,
            )

        def quantise(x16, name, width, fmt, pieces=1):
            codes = work.tile([P, width], U32, name=name, align_bytes=64)
            scales = work.tile([P, width], U8, name=name + "_s", align_bytes=64)
            n = width // pieces
            for i in range(pieces):
                cols = slice(i * n, (i + 1) * n)
                nc.vector.quantize_mx(
                    out=codes[:, cols].bitcast(fmt),
                    scales=scales[:, cols],
                    in_=x16[:, i * n * PLACES : (i + 1) * n * PLACES],
                )
            return codes, scales

        def quantise_v(b, g):
            v_mx[b, g] = quantise(v16[b, g], f"v{g}", N, E4M3)

        def quantise_do(b, g):
            do_mx[b, g] = quantise(do16[b, g], f"do{g}", NQ, E5M2)

        def quantise_qm(b):
            qm_mx[b] = quantise(qm16[b], "qm", D, E4M3)


        def dp_tile(b, t):
            dp = dp_pool.tile([P, N], F32, name="dp")
            cols = slice(t * P, (t + 1) * P)
            for g in range(PASSES):
                do_codes, do_scales = do_mx[b, g]
                v_codes, v_scales = v_mx[b, g]
                nc.tensor.matmul_mx(
                    out=dp[:],
                    lhsT=do_codes[:, cols].bitcast(E5M2),
                    lhsT_scale=do_scales[:, cols],
                    rhs=v_codes[:].bitcast(E4M3),
                    rhs_scale=v_scales[:],
                    start=(g == 0),
                    stop=(g == PASSES - 1),
                )
            return dp

        def ds_from_psum(b):
            ds = single.tile([P, PLACES, N], BF16, name="ds_rows", align_bytes=64)
            for t in range(PLACES):
                nc.vector.scalar_tensor_tensor(
                    out=ds[:, t, :],
                    in0=dp_tile(b, t)[:],
                    scalar=delta_t[:, b, t : t + 1],
                    in1=p_raw[b][:, t, :],
                    op0=SUBTRACT,
                    op1=MULTIPLY,
                )
            return ds

        def interleave(ds):
            ds16 = work.tile([P, N * PLACES], BF16, name="ds16", align_bytes=64)
            nc.vector.tensor_copy(
                ds16[:].rearrange("p (c i t) -> p c t i", t=PLACES, i=RUN), ds[:].rearrange("p t (c i) -> p c t i", i=RUN)
            )
            return ds16

        def dp_minus_delta(b):
            diff = single.tile([P, PLACES, N], F32, name="diff")
            for t in range(PLACES):
                nc.scalar.activation(diff[:, t, :], dp_tile(b, t)[:], IDENTITY, bias=minus_delta[:, b, t : t + 1])
            return diff

        def weigh(b, diff, pieces):
            ds16 = work.tile([P, N * PLACES], BF16, name="ds16", align_bytes=64)
            dst = ds16[:].rearrange("p (c i t) -> p c t i", t=PLACES, i=RUN)
            in0 = diff[:].rearrange("p t (c i) -> p c t i", i=RUN)
            in1 = p_raw[b][:].rearrange("p t (c i) -> p c t i", i=RUN)
            n = N // RUN // pieces
            for i in range(pieces):
                runs = slice(i * n, (i + 1) * n)
                nc.vector.tensor_tensor(dst[:, runs], in0[:, runs], in1[:, runs], MULTIPLY)
            return ds16

        def second_product(b, ds_mx, h, staged):
            dk = dk_pool.tile([P, N], F32, name="dk")
            cols = slice(h * P, (h + 1) * P)
            nc.tensor.matmul_mx(
                out=dk[:],
                lhsT=qm_mx[b][0][:, cols].bitcast(E4M3),
                lhsT_scale=qm_mx[b][1][:, cols],
                rhs=ds_mx[0][:].bitcast(E5M2),
                rhs_scale=ds_mx[1][:],
                start=True,
                stop=True,
            )
            nc.scalar.activation(staged[:], dk[:], COPY)

        def scatter(b, h, staged, piece=0, pieces=1):
            n = N // pieces
            first = b * LIST_COLS + piece * LIST_COLS // pieces
            nc.vector.tensor_copy(
                windows[b][h][:].indirect(offsets[:, first : first + LIST_COLS // pieces]),
                staged[:, piece * n : (piece + 1) * n],
            )

        def store(b, h):
            cols = slice(b * SEG, (b + 1) * SEG)
            nc.sync.dma_start(out[h * P : (h + 1) * P, cols], windows[b][h][:, cols])


        load_v(0, 0, 0)
        load_v(0, 0, 1)
        nc.sync.dma_start(delta_t[:], delta.rearrange("b (m t) o -> m b (t o)", t=PLACES))
        load_v(1, 0, 0)
        load_v(1, 0, 1)
        load_v(0, 1, 0, pieces=2)
        load_v(0, 1, 1)
        load_do(0, 0)
        load_do(0, 1)
        for b in range(B):
            for h in range(2):
                nc.gpsimd.memset(windows[b][h][:, b * SEG : (b + 1) * SEG], 0.0)
        nc.vector.tensor_scalar(minus_delta[:], delta_t[:], -1.0, None, MULTIPLY)

        round_v(0, 0, 0, vector_cols=SEG // 4)
        gather(0, 0, 0)
        round_v(0, 0, 1)
        gather(0, 0, 1)
        load_v(1, 1, 0)
        load_p(0)
        load_v(1, 1, 1)
        load_qm(0)
        load_do(1, 0)
        round_v(1, 0, 0)
        pack_v(0, 0)
        quantise_v(0, 0)
        gather(1, 0, 0)
        round_v(1, 0, 1)
        round_v(0, 1, 0, vector_cols=SEG // 4, lo=0, hi=SEG // 2)
        gather(1, 0, 1)
        round_v(0, 1, 0, vector_cols=SEG // 4, lo=SEG // 2, hi=SEG)
        pack_v(1, 0)
        gather(0, 1, 0)
        quantise_v(1, 0)
        round_v(0, 1, 1)
        gather(0, 1, 1)
        round_do(0, 0)
        load_do(1, 1)
        load_qm(1)
        load_p(1)
        pack_v(0, 1)
        quantise_v(0, 1)
        quantise_do(0, 0)
        round_do(0, 1, vector_cols=P // 4)
        quantise_do(0, 1)

        round_v(1, 1, 0, vector_cols=SEG // 2)
        gather(1, 1, 0)
        ds_rows = ds_from_psum(0)
        round_qm(0)
        ds16 = interleave(ds_rows)
        quantise_qm(0)
        ds_mx0 = quantise(ds16, "ds", N, E5M2)
        round_v(1, 1, 1)
        gather(1, 1, 1)
        round_do(1, 0, vector_cols=P // 4)
        pack_v(1, 1)
        quantise_v(1, 1)
        round_do(1, 1, vector_cols=P // 2)
        quantise_do(1, 0)

        staged00 = work.tile([P, N], F32, name="do16", align_bytes=64)
        second_product(0, ds_mx0, 0, staged00)
        scatter(0, 0, staged00, piece=0, pieces=2)
        quantise_do(1, 1)

        round_qm(1)
        diff = dp_minus_delta(1)
        quantise_qm(1)
        ds16 = weigh(1, diff, pieces=2)
        staged01 = work.tile([P, N], F32, name="do16", align_bytes=64)
        second_product(0, ds_mx0, 1, staged01)
        scatter(0, 0, staged00, piece=1, pieces=2)
        store(0, 0)
        scatter(0, 1, staged01, piece=0, pieces=2)
        ds_mx1 = quantise(ds16, "ds", N, E5M2, pieces=2)
        scatter(0, 1, staged01, piece=1, pieces=2)
        store(0, 1)

        staged1 = []
        for h in range(2):
            staged = work.tile([P, N], F32, name="staged")
            second_product(1, ds_mx1, h, staged)
            staged1.append(staged)
        for h in range(2):
            scatter(1, h, staged1[h])
            store(1, h)
